import numpy as np
import ml_dtypes


def mxq(x, axis, fmt="e4m3"):
    dtype, down = {"e4m3": (ml_dtypes.float8_e4m3fn, 7), "e5m2": (ml_dtypes.float8_e5m2, 14)}[fmt]
    v = np.moveaxis(np.asarray(x, np.float32).astype(ml_dtypes.bfloat16).astype(np.float64), axis, -1)
    blocks = v.reshape(v.shape[:-1] + (-1, 32))
    amax = np.abs(blocks).max(-1, keepdims=True)
    byte = np.maximum(np.where(amax > 0, np.frexp(amax)[1] - 1 + 127, 0) - down, 1)
    scale = np.exp2(byte - 127.0)
    codes = (blocks / scale).astype(np.float32).astype(dtype).astype(np.float64)
    return np.moveaxis((codes * scale).reshape(v.shape), -1, axis)


WIDE = False


def mx_kscale(k):
    if not WIDE:
        return np.ones(k)
    levels = np.array([10, -10, 5, -5, 0])
    if k % 512:
        return np.exp2(np.random.permutation(np.resize(levels, k // 32))).repeat(32)
    a = np.empty((k // 512, 16))
    for p in range(k // 512):
        a[p, :8] = np.random.permutation(np.resize(levels, 8))
        for g in range(8):
            far = levels[np.abs(levels - a[p, g]) >= 10]
            a[p, g + 8] = far[np.random.randint(len(far))]
    return np.exp2(a.ravel()).repeat(32)


def f64(x):
    return np.asarray(x).astype(np.float64)


def striped(idx):
    return np.tile(np.asarray(idx).reshape(-1, 16).T, (8, 1)).astype(np.uint16)


def unstriped(offs):
    return offs[:16].T.reshape(-1).astype(np.int64)


E2M1 = np.array([0.0, 0.5, 1.0, 1.5, 2.0, 3.0, 4.0, 6.0, -0.0, -0.5, -1.0, -1.5, -2.0, -3.0, -4.0, -6.0])


def pack_weight(w, fmt):
    k, n = w.shape
    w = f64(np.asarray(w, np.float32).astype(ml_dtypes.bfloat16)).reshape(k // 32, 32, n)
    amax = np.abs(w).max(1)
    if fmt == "e4m3":
        byte = np.frexp(amax)[1] - 1 + 127 - 7
    else:
        mant, ex = np.frexp(amax / 6.0)
        byte = np.where(mant > 0.5, ex, ex - 1) + 127
    byte = np.clip(np.where(amax > 0, byte, 1), 1, 254)
    scaled = (w * np.exp2(127.0 - byte)[:, None, :]).reshape(k, n).astype(np.float32)
    by_word = np.ascontiguousarray(scaled.reshape(k // 512, 128, 4, n).transpose(0, 1, 3, 2))
    if fmt == "e4m3":
        words = by_word.astype(ml_dtypes.float8_e4m3fn).view(np.uint8)
    else:
        c = by_word.astype(ml_dtypes.float4_e2m1fn).view(np.uint8) & 0xF
        words = (c[..., 0::2] | (c[..., 1::2] << 4)).reshape(k // 512, 128, 2 * n)
    return np.ascontiguousarray(words), np.ascontiguousarray(byte.astype(np.uint8).reshape(k // 512, 16, n))


def unpack_weight(words, scales, fmt):
    g, _, n = scales.shape
    words = np.ascontiguousarray(words).reshape(g, 128, n, -1)
    if fmt == "e4m3":
        vals = words.view(ml_dtypes.float8_e4m3fn).astype(np.float64)
    else:
        nib = np.empty((g, 128, n, 4), np.uint8)
        nib[..., 0::2] = words & 0xF
        nib[..., 1::2] = words >> 4
        vals = E2M1[nib]
    vals = vals * np.repeat(np.exp2(scales.astype(np.float64) - 127.0), 8, axis=1)[..., None]
    return vals.transpose(0, 1, 3, 2).reshape(g * 512, n)


def bf(x):
    return np.asarray(x, np.float32).astype(ml_dtypes.bfloat16)


def planes(Y):
    r, m = Y.shape
    b = f64(bf(Y)).reshape(r // 32, 32, m)
    amax = np.abs(b).max(1)
    byte = np.clip(np.where(amax > 0, np.frexp(amax)[1] - 1 + 127 - 7, 1), 1, 254)
    codes = (b * np.exp2(127.0 - byte)[:, None, :]).reshape(r, m).astype(np.float32).astype(ml_dtypes.float8_e4m3fn).view(np.uint8)
    words = codes.reshape(r // 512, 128, 4, m).transpose(0, 1, 3, 2)
    return np.ascontiguousarray(words), np.ascontiguousarray(byte.astype(np.uint8).reshape(r // 512, 16, m))


D, T, I, G, U, Q = 512, 4096, 1024, 64, 512, 512


def setup_inputs():
    n = np.random.standard_normal
    idx = np.random.permutation(T)[:I]
    idx2 = np.random.permutation(U)[:G]
    fd = mx_kscale(D)
    keysp = pack_weight(n((D, T)) / fd[:, None], "e2m1")
    return {
        "query": (n((D, Q)) * 1.0 / np.sqrt(D) * fd[:, None]).astype(np.float32),
        "keys_words": keysp[0],
        "keys_scales": keysp[1],
        "pquery": (n((D, Q)) * 1.0 / np.sqrt(D) * fd[:, None]).astype(np.float32),
        "pgsum": (n((D, U)) / fd[:, None]).astype(np.float32),
        "offs": striped(idx),
        "offs2": striped(idx2),
    }


def reference(query, keys_words, keys_scales, pquery, pgsum, offs, offs2):
    idx = unstriped(offs)
    idx2 = unstriped(offs2)
    keysu = unpack_weight(keys_words, keys_scales, "e2m1")
    queryq = mxq(f64(query), 0, "e4m3")
    keysidxg = keysu[:, idx]
    a = queryq.T @ keysidxg
    r = np.log(np.exp(a).reshape(Q, G, I // G).sum(axis=2))
    rf = np.zeros((Q, U))
    rf[:, idx2] = r
    pqueryq = mxq(f64(pquery), 0, "e4m3")
    pgsumq = mxq(f64(pgsum), 0, "e4m3")
    b = pqueryq.T @ pgsumq
    y = b + rf
    words, scales = planes(y)
    return y, words, scales

@@ -1,0 +1,179 @@
+from contextlib import ExitStack
+
+import concourse.mybir as mybir
+from concourse.masks import make_identity
+
+D, T, I, G, U, Q = 512, 4096, 1024, 64, 512, 512
+FLOPS = 2 * D * Q * (I + U)
+
+F32 = mybir.dt.float32
+BF16 = mybir.dt.bfloat16
+I32 = mybir.dt.int32
+U32 = mybir.dt.uint32
+U16 = mybir.dt.uint16
+U8 = mybir.dt.uint8
+FP8X4 = mybir.dt.float8_e4m3fn_x4
+FP4X4 = mybir.dt.float4_e2m1fn_x4
+ALU = mybir.AluOpType
+ACT = mybir.ActivationFunctionType
+AX = mybir.AxisListType
+
+P = 128
+PACK = 4
+PAGE = I // G
+BANK = 512
+HALVES = I // BANK
+GH = G // HALVES
+
+
+def tile_attend_pagelogsum_pl_kernel(tc, query, keys_words, keys_scales, pquery, pgsum, offs, offs2, out_0, out_1, out_2):
+    nc = tc.nc
+    with ExitStack() as ctx:
+        lists = ctx.enter_context(tc.tile_pool(name="lists", bufs=1))
+        keep = ctx.enter_context(tc.tile_pool(name="keep", bufs=1))
+        ring = ctx.enter_context(tc.tile_pool(name="ring", bufs=3))
+        mm = ctx.enter_context(tc.psum_pool(name="mm", bufs=6))
+        sums = ctx.enter_context(tc.psum_pool(name="sums", bufs=2))
+
+        slots = lists.tile([P, I // 16], U16, name="slots")
+        pages = lists.tile([P, G // 16], U16, name="pages")
+        kw = keep.tile([P, T], U16, name="kw", tag="wide0", align_bytes=64)
+        ks = keep.tile([P, T], U8, name="ks", tag="half", align_bytes=64)
+
+        def load_raw(src, tag):
+            raw = keep.tile([P, PACK, Q], F32, name="raw", tag=tag, align_bytes=64)
+            nc.sync.dma_start(out=raw[:], in_=src.rearrange("(p t) w -> p t w", t=PACK))
+            return raw
+
+        nc.gpsimd.memset(ks[:, 0 : T // 2].bitcast(I32), 0)
+        nc.vector.memset(ks[:, T // 2 : T].bitcast(I32), 0)
+        nc.sync.dma_start(out=kw[:].bitcast(I32), in_=keys_words[0].bitcast(I32))
+        nc.sync.dma_start(slots[:], offs)
+        for quad in range(4):
+            nc.scalar.dma_start(out=ks[32 * quad : 32 * quad + 4, :].bitcast(I32), in_=keys_scales[0, 4 * quad : 4 * quad + 4, :].bitcast(I32))
+        q_raw = load_raw(query, "wide1")
+        nc.sync.dma_start(pages[:], offs2)
+
+        ident = keep.tile([P, P], F32, name="ident")
+        make_identity(nc, ident[:])
+        rf = [keep.tile([P, U], F32, name="rf%d" % r) for r in range(PACK)]
+        for r in range(PACK):
+            nc.gpsimd.memset(rf[r][:], 0.0)
+
+        gs = keep.tile([P, I], U8, name="gs", align_bytes=64)
+        nc.vector.tensor_copy(gs[:], ks[:].indirect(slots[:]))
+        gw = keep.tile([P, I], U16, name="gw", tag="half", align_bytes=64)
+        nc.vector.tensor_copy(gw[:], kw[:].indirect(slots[:]))
+
+        def deal(raw, pr, name):
+            dst = keep.tile([P, 2, P, PACK], BF16, name=name, align_bytes=64)
+            nc.scalar.copy(
+                out=dst[:].rearrange("p r s t -> p s t r"),
+                in_=raw[:].rearrange("p t (s r) -> p s t r", r=PACK)[:, :, :, 2 * pr : 2 * pr + 2],
+            )
+            return dst[:].rearrange("p r s t -> p (r s t)")
+
+        def quantise(src_flat, name):
+            width = src_flat.shape[1] // PACK
+            codes = keep.tile([P, width], U32, name=name + "_codes", align_bytes=64)
+            scales = keep.tile([P, width], U8, name=name + "_scales", align_bytes=64)
+            nc.vector.quantize_mx(out=codes[:].bitcast(FP8X4), scales=scales[:], in_=src_flat)
+            return codes, scales
+
+        qb = [deal(q_raw, pr, "qb%d" % pr) for pr in range(2)]
+        qx = [quantise(qb[pr], "q%d" % pr) for pr in range(2)]
+        pq_raw = load_raw(pquery, "wide0")
+        pg_raw = load_raw(pgsum, "wide1")
+
+        top = [keep.tile([P, G], F32, name="top%d" % r) for r in range(PACK)]
+        e = [keep.tile([P, PAGE, P], F32, name="e%d" % pr) for pr in range(2)]
+        order = [(r, h) for r in range(PACK) for h in range(HALVES)]
+        banks = {}
+        diffs = {}
+
+        def score(r, h):
+            a = mm.tile([P, BANK], F32, name="acc")
+            nc.tensor.matmul_mx(
+                out=a[:],
+                lhsT=qx[r // 2][0][:, r % 2 * P : (r % 2 + 1) * P].bitcast(FP8X4),
+                lhsT_scale=qx[r // 2][1][:, r % 2 * P : (r % 2 + 1) * P],
+                rhs=gw[:, h * BANK : (h + 1) * BANK].bitcast(FP4X4),
+                rhs_scale=gs[:, h * BANK : (h + 1) * BANK],
+                start=True,
+                stop=True,
+            )
+            nc.vector.tensor_reduce(
+                out=top[r][:, h * GH : (h + 1) * GH], in_=a[:].rearrange("p (g j) -> p g j", j=PAGE), axis=AX.X, op=ALU.max
+            )
+            banks[(r, h)] = a
+
+        def weigh(r, h):
+            d = ring.tile([P, PAGE, GH], F32, name="diff")
+            nc.vector.tensor_tensor(
+                out=d[:],
+                in0=banks[(r, h)][:].rearrange("p (g j) -> p j g", j=PAGE),
+                in1=top[r][:, h * GH : (h + 1) * GH].unsqueeze(1).broadcast_to([P, PAGE, GH]),
+                op=ALU.subtract,
+            )
+            c0 = (r % 2) * G + h * GH
+            nc.scalar.activation(out=e[r // 2][:, :, c0 : c0 + GH], in_=d[:], func=ACT.Exp)
+            diffs[(r, h)] = d
+
+        turned = {}
+
+        def page_sums(pr, copy):
+            bank = sums.tile([P, 2 * P], F32, name="bank")
+            for j in range(PAGE):
+                nc.tensor.matmul(bank[:, 0:P], lhsT=e[pr][:, j, :], rhs=ident[:], is_transpose=True, start=(j == 0), stop=(j == PAGE - 1))
+            st = keep.tile([P, P], F32, name="st%d" % pr)
+            copy(out=st[:], in_=bank[:, 0:P])
+            nc.tensor.transpose(bank[:, P : 2 * P], st[:], ident[:])
+            turned[pr] = bank
+
+        score(*order[0])
+        for k in range(len(order)):
+            if k + 1 < len(order):
+                score(*order[k + 1])
+            weigh(*order[k])
+            if k == 3:
+                page_sums(0, nc.scalar.copy)
+
+        pgb = keep.tile([P, U, PACK], BF16, name="pgb", align_bytes=64)
+        nc.vector.tensor_copy(
+            out=pgb[:].rearrange("p (c i) t -> p c t i", i=4), in_=pg_raw[:].rearrange("p t (c i) -> p c t i", i=4)
+        )
+        pqx = [quantise(deal(pq_raw, pr, "pqb%d" % pr), "pq%d" % pr) for pr in range(2)]
+        pgc, pgs = quantise(pgb[:].rearrange("p u t -> p (u t)"), "pg")
+        page_sums(1, nc.vector.tensor_copy)
+
+        last = diffs[order[-1]][:].rearrange("p j g -> p (j g)")
+        y = keep.tile([P, PACK, U], F32, name="y")
+        out_rows = out_0.rearrange("(p r) u -> p r u", r=PACK)
+        for pr in range(2):
+            nc.scalar.activation(out=last[:, pr * P : (pr + 1) * P], in_=turned[pr][:, P : 2 * P], func=ACT.Ln)
+        for r in range(PACK):
+            b = mm.tile([P, U], F32, name="acc")
+            nc.tensor.matmul_mx(
+                out=b[:],
+                lhsT=pqx[r // 2][0][:, r % 2 * P : (r % 2 + 1) * P].bitcast(FP8X4),
+                lhsT_scale=pqx[r // 2][1][:, r % 2 * P : (r % 2 + 1) * P],
+                rhs=pgc[:].bitcast(FP8X4),
+                rhs_scale=pgs[:],
+                start=True,
+                stop=True,
+            )
+            nc.vector.tensor_tensor(rf[r][:].indirect(pages[:]), last[:, r * G : (r + 1) * G], top[r][:], ALU.add)
+            nc.vector.tensor_tensor(out=y[:, r, :], in0=b[:], in1=rf[r][:], op=ALU.add)
+            nc.sync.dma_start(out=out_rows[:, r, :], in_=y[:, r, :])
+
+        yb = keep.tile([P, U, PACK], BF16, name="yb", align_bytes=64)
+        split = 80
+        yb_v = yb[:].rearrange("p (c i) t -> p c t i", i=4)
+        y_v = y[:].rearrange("p t (c i) -> p c t i", i=4)
+        nc.vector.tensor_copy(out=yb_v[:, 0:split], in_=y_v[:, 0:split])
+        nc.scalar.copy(out=yb_v[:, split:], in_=y_v[:, split:])
+        yc, ys = quantise(yb[:].rearrange("p u t -> p (u t)"), "y")
+        nc.sync.dma_start(out=out_1[0].rearrange("p c r -> p (c r)").bitcast(I32), in_=yc[:].bitcast(I32))
+        for quad in range(4):
+            queue = nc.scalar if quad % 2 == 0 else nc.sync
+            queue.dma_start(out=out_2[0, 4 * quad : 4 * quad + 4, :].bitcast(I32), in_=ys[32 * quad : 32 * quad + 4, :].bitcast(I32))

@@ -1,7 +1,6 @@
 from contextlib import ExitStack
 
 import concourse.mybir as mybir
-from concourse.masks import make_identity
 
 D, T, I, G, U, Q = 512, 4096, 1024, 64, 512, 512
 FLOPS = 2 * D * Q * (I + U)
@@ -38,39 +37,49 @@ def tile_attend_pagelogsum_pl_kernel(tc, query, keys_words, keys_scales, pquery,
         slots = lists.tile([P, I // 16], U16, name="slots")
         pages = lists.tile([P, G // 16], U16, name="pages")
         kw = keep.tile([P, T], U16, name="kw", tag="wide0", align_bytes=64)
-        ks = keep.tile([P, T], U8, name="ks", tag="half", align_bytes=64)
+        ks = keep.tile([P, T], U8, name="ks", tag="wide2", align_bytes=64)
 
         def load_raw(src, tag):
             raw = keep.tile([P, PACK, Q], F32, name="raw", tag=tag, align_bytes=64)
             nc.sync.dma_start(out=raw[:], in_=src.rearrange("(p t) w -> p t w", t=PACK))
             return raw
 
-        nc.gpsimd.memset(ks[:, 0 : T // 2].bitcast(I32), 0)
-        nc.vector.memset(ks[:, T // 2 : T].bitcast(I32), 0)
-        nc.sync.dma_start(out=kw[:].bitcast(I32), in_=keys_words[0].bitcast(I32))
+        nc.vector.memset(ks[:].bitcast(I32), 0)
         nc.sync.dma_start(slots[:], offs)
+        nc.sync.dma_start(out=kw[:].bitcast(I32), in_=keys_words[0].bitcast(I32))
         for quad in range(4):
             nc.scalar.dma_start(out=ks[32 * quad : 32 * quad + 4, :].bitcast(I32), in_=keys_scales[0, 4 * quad : 4 * quad + 4, :].bitcast(I32))
-        q_raw = load_raw(query, "wide1")
-        nc.sync.dma_start(pages[:], offs2)
-
+        zeros = keep.tile([P, P], F32, name="zeros", tag="q1", align_bytes=64)
+        nc.vector.memset(zeros[:], 0.0)
         ident = keep.tile([P, P], F32, name="ident")
-        make_identity(nc, ident[:])
+        nc.gpsimd.affine_select(
+            out=ident[:], in_=zeros[:], compare_op=ALU.not_equal, fill=1.0, base=0, pattern=[[-1, P]], channel_multiplier=1
+        )
+        q_raw = [keep.tile([P, PACK, Q // 2], F32, name="q_raw", tag="q%d" % c, align_bytes=64) for c in range(2)]
+        for c in range(2):
+            nc.sync.dma_start(out=q_raw[c][:], in_=query.rearrange("(p t) w -> p t w", t=PACK)[:, :, c * Q // 2 : (c + 1) * Q // 2])
+        nc.sync.dma_start(pages[:], offs2)
         rf = [keep.tile([P, U], F32, name="rf%d" % r) for r in range(PACK)]
         for r in range(PACK):
-            nc.gpsimd.memset(rf[r][:], 0.0)
+            nc.vector.memset(rf[r][:], 0.0)
 
-        gs = keep.tile([P, I], U8, name="gs", align_bytes=64)
-        nc.vector.tensor_copy(gs[:], ks[:].indirect(slots[:]))
-        gw = keep.tile([P, I], U16, name="gw", tag="half", align_bytes=64)
+        gw = keep.tile([P, I], U16, name="gw", align_bytes=64)
         nc.vector.tensor_copy(gw[:], kw[:].indirect(slots[:]))
+        gs = {}
+        list_cols = BANK // 16
 
-        def deal(raw, pr, name):
-            dst = keep.tile([P, 2, P, PACK], BF16, name=name, align_bytes=64)
-            nc.scalar.copy(
-                out=dst[:].rearrange("p r s t -> p s t r"),
-                in_=raw[:].rearrange("p t (s r) -> p s t r", r=PACK)[:, :, :, 2 * pr : 2 * pr + 2],
-            )
+        def gather_scales(h, tag):
+            gs[h] = keep.tile([P, BANK], U8, name="gs", tag=tag, align_bytes=64)
+            nc.vector.tensor_copy(gs[h][:], ks[:].indirect(slots[:, h * list_cols : (h + 1) * list_cols]))
+
+        def deal(parts, pr, name):
+            dst = keep.tile([P, 2, P, PACK], BF16, name=name, tag=name, align_bytes=64)
+            n = P // len(parts)
+            for c, part in enumerate(parts):
+                nc.scalar.copy(
+                    out=dst[:].rearrange("p r s t -> p s t r")[:, c * n : (c + 1) * n],
+                    in_=part.rearrange("p t (s r) -> p s t r", r=PACK)[:, :, :, 2 * pr : 2 * pr + 2],
+                )
             return dst[:].rearrange("p r s t -> p (r s t)")
 
         def quantise(src_flat, name):
@@ -80,14 +89,17 @@ def tile_attend_pagelogsum_pl_kernel(tc, query, keys_words, keys_scales, pquery,
             nc.vector.quantize_mx(out=codes[:].bitcast(FP8X4), scales=scales[:], in_=src_flat)
             return codes, scales
 
-        qb = [deal(q_raw, pr, "qb%d" % pr) for pr in range(2)]
-        qx = [quantise(qb[pr], "q%d" % pr) for pr in range(2)]
-        pq_raw = load_raw(pquery, "wide0")
-        pg_raw = load_raw(pgsum, "wide1")
+        qb = [deal([part[:] for part in q_raw], pr, "qb%d" % pr) for pr in range(2)]
+        gather_scales(0, "gs0")
+        qx = [quantise(qb[0], "q0")]
+        gather_scales(1, "qb0")
+        qx.append(quantise(qb[1], "q1"))
+        pq_raw = load_raw(pquery, "q1")
+        pg_raw = load_raw(pgsum, "wide2")
 
         top = [keep.tile([P, G], F32, name="top%d" % r) for r in range(PACK)]
         e = [keep.tile([P, PAGE, P], F32, name="e%d" % pr) for pr in range(2)]
-        order = [(r, h) for r in range(PACK) for h in range(HALVES)]
+        order = [(2 * pr + rr, h) for pr in range(2) for h in range(HALVES) for rr in range(2)]
         banks = {}
         diffs = {}
 
@@ -98,7 +110,7 @@ def tile_attend_pagelogsum_pl_kernel(tc, query, keys_words, keys_scales, pquery,
                 lhsT=qx[r // 2][0][:, r % 2 * P : (r % 2 + 1) * P].bitcast(FP8X4),
                 lhsT_scale=qx[r // 2][1][:, r % 2 * P : (r % 2 + 1) * P],
                 rhs=gw[:, h * BANK : (h + 1) * BANK].bitcast(FP4X4),
-                rhs_scale=gs[:, h * BANK : (h + 1) * BANK],
+                rhs_scale=gs[h][:],
                 start=True,
                 stop=True,
             )
@@ -108,15 +120,15 @@ def tile_attend_pagelogsum_pl_kernel(tc, query, keys_words, keys_scales, pquery,
             banks[(r, h)] = a
 
         def weigh(r, h):
-            d = ring.tile([P, PAGE, GH], F32, name="diff")
+            d = ring.tile([P, PAGE // 2, GH, 2], F32, name="diff")
             nc.vector.tensor_tensor(
                 out=d[:],
-                in0=banks[(r, h)][:].rearrange("p (g j) -> p j g", j=PAGE),
-                in1=top[r][:, h * GH : (h + 1) * GH].unsqueeze(1).broadcast_to([P, PAGE, GH]),
+                in0=banks[(r, h)][:].rearrange("p (g jj two) -> p jj g two", g=GH, two=2),
+                in1=top[r][:, h * GH : (h + 1) * GH].unsqueeze(1).unsqueeze(3).broadcast_to([P, PAGE // 2, GH, 2]),
                 op=ALU.subtract,
             )
             c0 = (r % 2) * G + h * GH
-            nc.scalar.activation(out=e[r // 2][:, :, c0 : c0 + GH], in_=d[:], func=ACT.Exp)
+            nc.scalar.activation(out=e[r // 2][:, :, c0 : c0 + GH].rearrange("p (jj two) g -> p jj two g", two=2), in_=d[:].rearrange("p jj g two -> p jj two g"), func=ACT.Exp)
             diffs[(r, h)] = d
 
         turned = {}
@@ -142,11 +154,11 @@ def tile_attend_pagelogsum_pl_kernel(tc, query, keys_words, keys_scales, pquery,
         nc.vector.tensor_copy(
             out=pgb[:].rearrange("p (c i) t -> p c t i", i=4), in_=pg_raw[:].rearrange("p t (c i) -> p c t i", i=4)
         )
-        pqx = [quantise(deal(pq_raw, pr, "pqb%d" % pr), "pq%d" % pr) for pr in range(2)]
+        pqx = [quantise(deal([pq_raw[:, :, 0 : Q // 2], pq_raw[:, :, Q // 2 : Q]], pr, "pqb%d" % pr), "pq%d" % pr) for pr in range(2)]
         pgc, pgs = quantise(pgb[:].rearrange("p u t -> p (u t)"), "pg")
         page_sums(1, nc.vector.tensor_copy)
 
-        last = diffs[order[-1]][:].rearrange("p j g -> p (j g)")
+        last = diffs[order[-1]][:].rearrange("p jj g two -> p (jj g two)")
         y = keep.tile([P, PACK, U], F32, name="y")
         out_rows = out_0.rearrange("(p r) u -> p r u", r=PACK)
         for pr in range(2):
@@ -167,7 +179,7 @@ def tile_attend_pagelogsum_pl_kernel(tc, query, keys_words, keys_scales, pquery,
             nc.sync.dma_start(out=out_rows[:, r, :], in_=y[:, r, :])
 
         yb = keep.tile([P, U, PACK], BF16, name="yb", align_bytes=64)
-        split = 80
+        split = 88
         yb_v = yb[:].rearrange("p (c i) t -> p c t i", i=4)
         y_v = y[:].rearrange("p t (c i) -> p c t i", i=4)
         nc.vector.tensor_copy(out=yb_v[:, 0:split], in_=y_v[:, 0:split])

from contextlib import ExitStack

import concourse.mybir as mybir

D, T, I, G, U, Q = 512, 4096, 1024, 64, 512, 512
FLOPS = 2 * D * Q * (I + U)

F32 = mybir.dt.float32
BF16 = mybir.dt.bfloat16
I32 = mybir.dt.int32
U32 = mybir.dt.uint32
U16 = mybir.dt.uint16
U8 = mybir.dt.uint8
FP8X4 = mybir.dt.float8_e4m3fn_x4
FP4X4 = mybir.dt.float4_e2m1fn_x4
ALU = mybir.AluOpType
ACT = mybir.ActivationFunctionType
AX = mybir.AxisListType

P = 128
PACK = 4
PAGE = I // G
BANK = 512
HALVES = I // BANK
GH = G // HALVES


def tile_attend_pagelogsum_pl_kernel(tc, query, keys_words, keys_scales, pquery, pgsum, offs, offs2, out_0, out_1, out_2):
    nc = tc.nc
    with ExitStack() as ctx:
        lists = ctx.enter_context(tc.tile_pool(name="lists", bufs=1))
        keep = ctx.enter_context(tc.tile_pool(name="keep", bufs=1))
        ring = ctx.enter_context(tc.tile_pool(name="ring", bufs=3))
        mm = ctx.enter_context(tc.psum_pool(name="mm", bufs=6))
        sums = ctx.enter_context(tc.psum_pool(name="sums", bufs=2))

        slots = lists.tile([P, I // 16], U16, name="slots")
        pages = lists.tile([P, G // 16], U16, name="pages")
        kw = keep.tile([P, T], U16, name="kw", tag="wide0", align_bytes=64)
        ks = keep.tile([P, T], U8, name="ks", tag="wide2", align_bytes=64)

        def load_raw(src, tag):
            raw = keep.tile([P, PACK, Q], F32, name="raw", tag=tag, align_bytes=64)
            nc.sync.dma_start(out=raw[:], in_=src.rearrange("(p t) w -> p t w", t=PACK))
            return raw

        nc.vector.memset(ks[:].bitcast(I32), 0)
        nc.sync.dma_start(slots[:], offs)
        nc.sync.dma_start(out=kw[:].bitcast(I32), in_=keys_words[0].bitcast(I32))
        for quad in range(4):
            nc.scalar.dma_start(out=ks[32 * quad : 32 * quad + 4, :].bitcast(I32), in_=keys_scales[0, 4 * quad : 4 * quad + 4, :].bitcast(I32))
        zeros = keep.tile([P, P], F32, name="zeros", tag="q1", align_bytes=64)
        nc.vector.memset(zeros[:], 0.0)
        ident = keep.tile([P, P], F32, name="ident")
        nc.gpsimd.affine_select(
            out=ident[:], in_=zeros[:], compare_op=ALU.not_equal, fill=1.0, base=0, pattern=[[-1, P]], channel_multiplier=1
        )
        q_raw = [keep.tile([P, PACK, Q // 2], F32, name="q_raw", tag="q%d" % c, align_bytes=64) for c in range(2)]
        for c in range(2):
            nc.sync.dma_start(out=q_raw[c][:], in_=query.rearrange("(p t) w -> p t w", t=PACK)[:, :, c * Q // 2 : (c + 1) * Q // 2])
        nc.sync.dma_start(pages[:], offs2)
        rf = [keep.tile([P, U], F32, name="rf%d" % r) for r in range(PACK)]
        for r in range(PACK):
            nc.vector.memset(rf[r][:], 0.0)

        gw = keep.tile([P, I], U16, name="gw", align_bytes=64)
        nc.vector.tensor_copy(gw[:], kw[:].indirect(slots[:]))
        gs = {}
        list_cols = BANK // 16

        def gather_scales(h, tag):
            gs[h] = keep.tile([P, BANK], U8, name="gs", tag=tag, align_bytes=64)
            nc.vector.tensor_copy(gs[h][:], ks[:].indirect(slots[:, h * list_cols : (h + 1) * list_cols]))

        def deal(parts, pr, name):
            dst = keep.tile([P, 2, P, PACK], BF16, name=name, tag=name, align_bytes=64)
            n = P // len(parts)
            for c, part in enumerate(parts):
                nc.scalar.copy(
                    out=dst[:].rearrange("p r s t -> p s t r")[:, c * n : (c + 1) * n],
                    in_=part.rearrange("p t (s r) -> p s t r", r=PACK)[:, :, :, 2 * pr : 2 * pr + 2],
                )
            return dst[:].rearrange("p r s t -> p (r s t)")

        def quantise(src_flat, name):
            width = src_flat.shape[1] // PACK
            codes = keep.tile([P, width], U32, name=name + "_codes", align_bytes=64)
            scales = keep.tile([P, width], U8, name=name + "_scales", align_bytes=64)
            nc.vector.quantize_mx(out=codes[:].bitcast(FP8X4), scales=scales[:], in_=src_flat)
            return codes, scales

        qb = [deal([part[:] for part in q_raw], pr, "qb%d" % pr) for pr in range(2)]
        gather_scales(0, "gs0")
        qx = [quantise(qb[0], "q0")]
        gather_scales(1, "qb0")
        qx.append(quantise(qb[1], "q1"))
        pq_raw = load_raw(pquery, "q1")
        pg_raw = load_raw(pgsum, "wide2")

        top = [keep.tile([P, G], F32, name="top%d" % r) for r in range(PACK)]
        e = [keep.tile([P, PAGE, P], F32, name="e%d" % pr) for pr in range(2)]
        order = [(2 * pr + rr, h) for pr in range(2) for h in range(HALVES) for rr in range(2)]
        banks = {}
        diffs = {}

        def score(r, h):
            a = mm.tile([P, BANK], F32, name="acc")
            nc.tensor.matmul_mx(
                out=a[:],
                lhsT=qx[r // 2][0][:, r % 2 * P : (r % 2 + 1) * P].bitcast(FP8X4),
                lhsT_scale=qx[r // 2][1][:, r % 2 * P : (r % 2 + 1) * P],
                rhs=gw[:, h * BANK : (h + 1) * BANK].bitcast(FP4X4),
                rhs_scale=gs[h][:],
                start=True,
                stop=True,
            )
            nc.vector.tensor_reduce(
                out=top[r][:, h * GH : (h + 1) * GH], in_=a[:].rearrange("p (g j) -> p g j", j=PAGE), axis=AX.X, op=ALU.max
            )
            banks[(r, h)] = a

        def weigh(r, h):
            d = ring.tile([P, PAGE // 2, GH, 2], F32, name="diff")
            nc.vector.tensor_tensor(
                out=d[:],
                in0=banks[(r, h)][:].rearrange("p (g jj two) -> p jj g two", g=GH, two=2),
                in1=top[r][:, h * GH : (h + 1) * GH].unsqueeze(1).unsqueeze(3).broadcast_to([P, PAGE // 2, GH, 2]),
                op=ALU.subtract,
            )
            c0 = (r % 2) * G + h * GH
            nc.scalar.activation(out=e[r // 2][:, :, c0 : c0 + GH].rearrange("p (jj two) g -> p jj two g", two=2), in_=d[:].rearrange("p jj g two -> p jj two g"), func=ACT.Exp)
            diffs[(r, h)] = d

        turned = {}

        def page_sums(pr, copy):
            bank = sums.tile([P, 2 * P], F32, name="bank")
            for j in range(PAGE):
                nc.tensor.matmul(bank[:, 0:P], lhsT=e[pr][:, j, :], rhs=ident[:], is_transpose=True, start=(j == 0), stop=(j == PAGE - 1))
            st = keep.tile([P, P], F32, name="st%d" % pr)
            copy(out=st[:], in_=bank[:, 0:P])
            nc.tensor.transpose(bank[:, P : 2 * P], st[:], ident[:])
            turned[pr] = bank

        score(*order[0])
        for k in range(len(order)):
            if k + 1 < len(order):
                score(*order[k + 1])
            weigh(*order[k])
            if k == 3:
                page_sums(0, nc.scalar.copy)

        pgb = keep.tile([P, U, PACK], BF16, name="pgb", align_bytes=64)
        nc.vector.tensor_copy(
            out=pgb[:].rearrange("p (c i) t -> p c t i", i=4), in_=pg_raw[:].rearrange("p t (c i) -> p c t i", i=4)
        )
        pqx = [quantise(deal([pq_raw[:, :, 0 : Q // 2], pq_raw[:, :, Q // 2 : Q]], pr, "pqb%d" % pr), "pq%d" % pr) for pr in range(2)]
        pgc, pgs = quantise(pgb[:].rearrange("p u t -> p (u t)"), "pg")
        page_sums(1, nc.vector.tensor_copy)

        last = diffs[order[-1]][:].rearrange("p jj g two -> p (jj g two)")
        y = keep.tile([P, PACK, U], F32, name="y")
        out_rows = out_0.rearrange("(p r) u -> p r u", r=PACK)
        for pr in range(2):
            nc.scalar.activation(out=last[:, pr * P : (pr + 1) * P], in_=turned[pr][:, P : 2 * P], func=ACT.Ln)
        for r in range(PACK):
            b = mm.tile([P, U], F32, name="acc")
            nc.tensor.matmul_mx(
                out=b[:],
                lhsT=pqx[r // 2][0][:, r % 2 * P : (r % 2 + 1) * P].bitcast(FP8X4),
                lhsT_scale=pqx[r // 2][1][:, r % 2 * P : (r % 2 + 1) * P],
                rhs=pgc[:].bitcast(FP8X4),
                rhs_scale=pgs[:],
                start=True,
                stop=True,
            )
            nc.vector.tensor_tensor(rf[r][:].indirect(pages[:]), last[:, r * G : (r + 1) * G], top[r][:], ALU.add)
            nc.vector.tensor_tensor(out=y[:, r, :], in0=b[:], in1=rf[r][:], op=ALU.add)
            nc.sync.dma_start(out=out_rows[:, r, :], in_=y[:, r, :])

        yb = keep.tile([P, U, PACK], BF16, name="yb", align_bytes=64)
        split = 88
        yb_v = yb[:].rearrange("p (c i) t -> p c t i", i=4)
        y_v = y[:].rearrange("p t (c i) -> p c t i", i=4)
        nc.vector.tensor_copy(out=yb_v[:, 0:split], in_=y_v[:, 0:split])
        nc.scalar.copy(out=yb_v[:, split:], in_=y_v[:, split:])
        yc, ys = quantise(yb[:].rearrange("p u t -> p (u t)"), "y")
        nc.sync.dma_start(out=out_1[0].rearrange("p c r -> p (c r)").bitcast(I32), in_=yc[:].bitcast(I32))
        for quad in range(4):
            queue = nc.scalar if quad % 2 == 0 else nc.sync
            queue.dma_start(out=out_2[0, 4 * quad : 4 * quad + 4, :].bitcast(I32), in_=ys[32 * quad : 32 * quad + 4, :].bitcast(I32))
